import numpy as np
import ml_dtypes


def mxq(x, axis, fmt="e4m3"):
    dtype, down = {"e4m3": (ml_dtypes.float8_e4m3fn, 7), "e5m2": (ml_dtypes.float8_e5m2, 14)}[fmt]
    v = np.moveaxis(np.asarray(x, np.float32).astype(ml_dtypes.bfloat16).astype(np.float64), axis, -1)
    blocks = v.reshape(v.shape[:-1] + (-1, 32))
    amax = np.abs(blocks).max(-1, keepdims=True)
    byte = np.maximum(np.where(amax > 0, np.frexp(amax)[1] - 1 + 127, 0) - down, 1)
    scale = np.exp2(byte - 127.0)
    codes = (blocks / scale).astype(np.float32).astype(dtype).astype(np.float64)
    return np.moveaxis((codes * scale).reshape(v.shape), -1, axis)


WIDE = False


def mx_kscale(k):
    if not WIDE:
        return np.ones(k)
    levels = np.array([10, -10, 5, -5, 0])
    if k % 512:
        return np.exp2(np.random.permutation(np.resize(levels, k // 32))).repeat(32)
    a = np.empty((k // 512, 16))
    for p in range(k // 512):
        a[p, :8] = np.random.permutation(np.resize(levels, 8))
        for g in range(8):
            far = levels[np.abs(levels - a[p, g]) >= 10]
            a[p, g + 8] = far[np.random.randint(len(far))]
    return np.exp2(a.ravel()).repeat(32)


def f64(x):
    return np.asarray(x).astype(np.float64)


def striped(idx):
    return np.tile(idx.reshape(-1, 16).T, (8, 1)).astype(np.uint16)


def unstriped(offs):
    return offs[:16].T.reshape(-1).astype(np.int64)


E2M1 = np.array([0.0, 0.5, 1.0, 1.5, 2.0, 3.0, 4.0, 6.0, -0.0, -0.5, -1.0, -1.5, -2.0, -3.0, -4.0, -6.0])


def pack_weight(w, fmt):
    k, n = w.shape
    w = f64(np.asarray(w, np.float32).astype(ml_dtypes.bfloat16)).reshape(k // 32, 32, n)
    amax = np.abs(w).max(1)
    if fmt == "e4m3":
        byte = np.frexp(amax)[1] - 1 + 127 - 7
    else:
        mant, ex = np.frexp(amax / 6.0)
        byte = np.where(mant > 0.5, ex, ex - 1) + 127
    byte = np.clip(np.where(amax > 0, byte, 1), 1, 254)
    scaled = (w * np.exp2(127.0 - byte)[:, None, :]).reshape(k, n).astype(np.float32)
    by_word = np.ascontiguousarray(scaled.reshape(k // 512, 128, 4, n).transpose(0, 1, 3, 2))
    if fmt == "e4m3":
        words = by_word.astype(ml_dtypes.float8_e4m3fn).view(np.uint8)
    else:
        c = by_word.astype(ml_dtypes.float4_e2m1fn).view(np.uint8) & 0xF
        words = (c[..., 0::2] | (c[..., 1::2] << 4)).reshape(k // 512, 128, 2 * n)
    return np.ascontiguousarray(words), np.ascontiguousarray(byte.astype(np.uint8).reshape(k // 512, 16, n))


def unpack_weight(words, scales, fmt):
    g, _, n = scales.shape
    words = np.ascontiguousarray(words).reshape(g, 128, n, -1)
    if fmt == "e4m3":
        vals = words.view(ml_dtypes.float8_e4m3fn).astype(np.float64)
    else:
        nib = np.empty((g, 128, n, 4), np.uint8)
        nib[..., 0::2] = words & 0xF
        nib[..., 1::2] = words >> 4
        vals = E2M1[nib]
    vals = vals * np.repeat(np.exp2(scales.astype(np.float64) - 127.0), 8, axis=1)[..., None]
    return vals.transpose(0, 1, 3, 2).reshape(g * 512, n)


def gelu(v):
    return 0.5 * v * (1.0 + np.tanh(np.sqrt(2.0 / np.pi) * (v + 0.044715 * v**3)))


K, T, S, H, P, N = 1536, 4096, 1024, 1024, 512, 768

def setup_inputs():
    n = np.random.standard_normal
    s = mx_kscale(K)[:, None]
    u = mx_kscale(H)[:, None]
    d = {}
    d["tab_words"], d["tab_scales"] = pack_weight(n((K, T)) * s, "e2m1")
    d["offs"] = striped(np.random.permutation(T)[:S])
    d["w1"] = (1.5 * n((K, H)) / K ** 0.5 / s).astype(np.float32)
    d["gain"] = (np.exp(0.3 * n(H)) * u[:, 0]).astype(np.float32)
    d["pos1"] = striped(np.random.permutation(S)[:P])
    d["pos2"] = striped(np.random.permutation(S)[:P])
    d["margin"] = (0.7 * n((H, P)) * u).astype(np.float32)
    d["w4_words"], d["w4_scales"] = pack_weight(n((H, N)) / H ** 0.5 / u, "e2m1")
    return d

def reference(tab_words, tab_scales, offs, w1, gain, pos1, pos2, margin, w4_words, w4_scales):
    v = unpack_weight(tab_words, tab_scales, "e2m1")[:, unstriped(offs)]
    w4 = unpack_weight(w4_words, w4_scales, "e2m1")
    pre = mxq(f64(w1), 0, "e4m3").T @ v
    h = f64(gain)[:, None] * np.tanh(pre)
    diff = h[:, unstriped(pos1)] - h[:, unstriped(pos2)]
    z = np.maximum(diff, f64(margin))
    return w4.T @ mxq(z, 0, "e4m3")

@@ -1,0 +1,332 @@
+from contextlib import ExitStack
+
+import concourse.mybir as mybir
+
+K, T, S, H, NCMP, N = 1536, 4096, 1024, 1024, 512, 768
+FLOPS = 2 * K * H * S + 2 * H * N * NCMP
+
+F32 = mybir.dt.float32
+BF16 = mybir.dt.bfloat16
+I32 = mybir.dt.int32
+U32 = mybir.dt.uint32
+U16 = mybir.dt.uint16
+U8 = mybir.dt.uint8
+FP8X4 = mybir.dt.float8_e4m3fn_x4
+FP4X4 = mybir.dt.float4_e2m1fn_x4
+ALU = mybir.AluOpType
+TANH = mybir.ActivationFunctionType.Tanh
+
+P = 128
+PASSES = K // 512
+BANK = 512
+HEAD_COLS = 384
+MOVED_ROWS = 112
+GROUPS = ((0, 2), (256, 2), (512, 4))
+
+
+def tile_list_punch_station_margins_kernel(
+    tc, tab_words, tab_scales, offs, w1, gain, pos1, pos2, margin, w4_words, w4_scales, out
+):
+    nc = tc.nc
+    with ExitStack() as ctx:
+        lists = ctx.enter_context(tc.tile_pool(name="lists", bufs=1))
+        keep = ctx.enter_context(tc.tile_pool(name="keep", bufs=1))
+        psum = ctx.enter_context(tc.psum_pool(name="psum", bufs=1))
+
+        places = {}
+        used = [0]
+
+        def held(shape, dtype, name, room=0, on=None, skip=0):
+            size = math_size(shape, dtype)
+            if on is None:
+                start, space = used[0], max(size, room)
+                used[0] = start + (space + 63) // 64 * 64
+            else:
+                start, space = places[on][0] + skip, places[on][1] - skip
+                assert size <= space, name
+            places[name] = (start, space if skip or on is None else space)
+            return keep.tile(shape, dtype, name=name, offset=start, align_bytes=64)
+
+        offs_t = lists.tile([P, S // 16], U16, name="offs_t")
+        pos1_t = lists.tile([P, NCMP // 16], U16, name="pos1_t")
+        pos2_t = lists.tile([P, NCMP // 16], U16, name="pos2_t")
+
+        tab = [held([P, T], U16, f"tab{a}") for a in range(PASSES)]
+        tab_sc = held([P, T], U8, "tab_sc")
+        nc.vector.memset(tab_sc[:].bitcast(I32), 0)
+        for q in range(4):
+            nc.gpsimd.dma_start(
+                out=tab_sc[32 * q : 32 * q + 4 * PASSES, :].bitcast(I32),
+                in_=tab_scales[:, 4 * q : 4 * q + 4, :].bitcast(I32),
+            )
+        warm = held([P, 8], F32, "warm")
+        nc.vector.memset(warm[:], 0.0)
+        warm_out = held([P, 8], F32, "warm_out")
+        nc.scalar.activation(out=warm_out[:], in_=warm[:], func=TANH)
+        planes = [held([P, S], U8, f"plane{a}") for a in range(PASSES)]
+        for a in range(1, PASSES):
+            nc.vector.memset(planes[a][:].bitcast(I32), 0)
+        w4_sc = held([P, 2, N], U8, "w4_sc")
+        nc.vector.memset(w4_sc[:].rearrange("p a n -> p (a n)").bitcast(I32), 0)
+
+        w_raw = {}
+
+        def load_tab(a):
+            nc.sync.dma_start(out=tab[a][:].bitcast(I32), in_=tab_words[a].bitcast(I32))
+
+        def load_w(g, a, parts=1):
+            c0, nt = GROUPS[g]
+            width = nt * P // parts
+            w_raw[g, a] = []
+            for k in range(parts):
+                raw = held([P, 4, width], F32, f"w_raw{g}_{a}_{k}")
+                rows = w1[512 * a : 512 * (a + 1), c0 + k * width : c0 + (k + 1) * width]
+                nc.sync.dma_start(out=raw[:], in_=rows.rearrange("(p j) c -> p j c", j=4))
+                w_raw[g, a].append(raw)
+
+        marg = {}
+
+        def load_margin(g):
+            c0, nt = GROUPS[g]
+            marg[g] = held([P, nt, NCMP], F32, f"marg{g}")
+            nc.sync.dma_start(out=marg[g][:], in_=margin[c0 : c0 + nt * P, :].rearrange("(p u) j -> p u j", u=nt))
+
+        nc.sync.dma_start(offs_t[:], offs)
+        load_tab(0)
+        load_w(0, 0)
+        load_tab(1)
+        load_w(0, 1)
+        load_w(0, 2)
+        load_tab(2)
+        load_w(1, 0)
+        nc.sync.dma_start(pos2_t[:], pos2)
+        nc.sync.dma_start(pos1_t[:], pos1)
+        gain_low = held([P, 2, 2], F32, "gain_low")
+        nc.sync.dma_start(out=gain_low[:], in_=gain[0:512].rearrange("(g p u) -> p g u", g=2, u=2))
+        load_w(1, 1)
+        load_margin(0)
+        load_w(1, 2)
+        load_w(2, 0)
+        load_w(2, 1)
+        load_margin(1)
+        load_w(2, 2, 2)
+        gain_high = held([P, 4], F32, "gain_high")
+        nc.sync.dma_start(out=gain_high[:], in_=gain[512:1024].rearrange("(p u) -> p u", u=4))
+        gains = [gain_low[:, 0, :], gain_low[:, 1, :], gain_high[:]]
+        load_margin(2)
+        w4 = held([P, 2, 2 * N], U8, "w4")
+        nc.sync.dma_start(out=w4[:].bitcast(I32), in_=w4_words.bitcast(I32).rearrange("a p c -> p a c"))
+        for q in range(4):
+            nc.sync.dma_start(
+                out=w4_sc[32 * q : 32 * q + 4].bitcast(I32),
+                in_=w4_scales[:, 4 * q : 4 * q + 4, :].bitcast(I32).rearrange("a r c -> r a c"),
+            )
+
+        v = {}
+
+        def gather_words(a, s0, s1, on=None):
+            got = held([P, (s1 - s0) * BANK], U16, f"v{a}_{s0}", on=on)
+            nc.vector.tensor_copy(out=got[:], in_=tab[a][:].indirect(offs_t[:, 32 * s0 : 32 * s1]))
+            for s in range(s0, s1):
+                v[a, s] = got[:, (s - s0) * BANK : (s - s0 + 1) * BANK]
+
+        wb, codes, scales = {}, {}, {}
+
+        def cast_w(g, a, on=None, skip=0):
+            nt = GROUPS[g][1]
+            wb[g, a] = held([P, nt * 512], BF16, f"wb{g}_{a}", on=on, skip=skip)
+            if nt == 2:
+                dst = wb[g, a][:].rearrange("p (u m e j) -> p m j e u", u=2, e=2, j=4)
+                nc.scalar.copy(out=dst, in_=w_raw[g, a][0][:].rearrange("p j (m e u) -> p m j e u", e=2, u=2))
+            else:
+                dst = wb[g, a][:].rearrange("p (u m j) -> p m j u", u=4, j=4)
+                rows = P // len(w_raw[g, a])
+                for k, raw in enumerate(w_raw[g, a]):
+                    nc.scalar.copy(out=dst[:, k * rows : (k + 1) * rows], in_=raw[:].rearrange("p j (m u) -> p m j u", u=4))
+
+        def quantize_w(g, a, on=None):
+            nt = GROUPS[g][1]
+            codes[g, a] = held([P, nt * P], U32, f"codes{g}_{a}", room=4096, on=on)
+            scales[g, a] = held([P, nt * P], U8, f"scales{g}_{a}", room=1024)
+            nc.vector.quantize_mx(out=codes[g, a][:].bitcast(FP8X4), scales=scales[g, a][:], in_=wb[g, a][:])
+
+        banks = [0]
+        hs = {}
+
+        def read_tile(g, u, on=None):
+            hs[g, u] = held([P, S], F32, f"h{g}_{u}", on=on)
+            for s in range(2):
+                acc = psum.tile([P, BANK], F32, name="acc", tag=f"bank{banks[0] % 8}")
+                banks[0] = banks[0] + 1
+                for a in range(PASSES):
+                    nc.tensor.matmul_mx(
+                        out=acc[:],
+                        lhsT=codes[g, a][:, u * P : (u + 1) * P].bitcast(FP8X4),
+                        lhsT_scale=scales[g, a][:, u * P : (u + 1) * P],
+                        rhs=v[a, s].bitcast(FP4X4),
+                        rhs_scale=planes[a][:, s * BANK : (s + 1) * BANK],
+                        start=(a == 0),
+                        stop=(a == PASSES - 1),
+                    )
+                nc.scalar.activation(out=hs[g, u][:, s * BANK : (s + 1) * BANK], in_=acc[:], func=TANH)
+
+        second, diff = {}, {}
+
+        def pick_second(g, u, j0, j1, on=None):
+            second[g, u, j0] = held([P, j1 - j0], F32, f"second{g}_{u}_{j0}", on=on)
+            nc.vector.tensor_copy(out=second[g, u, j0][:], in_=hs[g, u][:].indirect(pos2_t[:, j0 // 16 : j1 // 16]))
+
+        def subtract(g, u, j0, j1):
+            diff[g, u, j0] = held([P, j1 - j0], F32, f"diff{g}_{u}_{j0}")
+            nc.vector.tensor_tensor(
+                diff[g, u, j0][:], hs[g, u][:].indirect(pos1_t[:, j0 // 16 : j1 // 16]), second[g, u, j0][:], ALU.subtract
+            )
+
+        def floor(g, u, j0, j1, z):
+            nc.vector.scalar_tensor_tensor(
+                out=z,
+                in0=diff[g, u, j0][:],
+                scalar=gains[g][:, u : u + 1],
+                in1=marg[g][:, u, j0:j1],
+                op0=ALU.mult,
+                op1=ALU.max,
+            )
+
+        def weave(z, width, engine_copy, name, on=None):
+            woven = held([P, 4 * width], BF16, name, on=on)
+            engine_copy(
+                out=woven[:].rearrange("p (c i t) -> p c t i", i=4, t=4),
+                in_=z.rearrange("p t (c i) -> p c t i", i=4),
+            )
+            return woven
+
+        def quantize_z(woven, width, name):
+            zc = held([P, width], U32, f"zc{name}")
+            zs = held([P, width], U8, f"zs{name}")
+            c0 = 0
+            while c0 < width:
+                step = 512 if width - c0 >= 512 else (256 if width - c0 >= 256 else 128)
+                nc.vector.quantize_mx(
+                    out=zc[:, c0 : c0 + step].bitcast(FP8X4),
+                    scales=zs[:, c0 : c0 + step],
+                    in_=woven[:, 4 * c0 : 4 * (c0 + step)],
+                )
+                c0 = c0 + step
+            return zc, zs
+
+        z0 = held([P, 4, NCMP], BF16, "z0")
+
+        def floor_and_move(g, u, on=None):
+            z = held([P, NCMP], BF16, f"z{g}_{u}", on=on)
+            floor(g, u, 0, NCMP, z[:])
+            for e in range(2):
+                nc.gpsimd.dma_start(out=z0[64 * g : 64 * g + 64, 2 * e + u, :], in_=z[e:P:2, :])
+
+        gather_words(0, 0, 2)
+        nc.vector.tensor_copy(out=planes[0][:], in_=tab_sc[:].indirect(offs_t[:]))
+        for a in range(1, PASSES):
+            nc.gpsimd.dma_start(
+                out=planes[a][0:MOVED_ROWS, :].bitcast(I32),
+                in_=planes[0][4 * a : 4 * a + MOVED_ROWS, :].bitcast(I32),
+            )
+        cast_w(0, 0)
+        quantize_w(0, 0)
+        gather_words(1, 0, 2, on="tab_sc")
+        for a in (1, 2):
+            cast_w(0, a)
+            quantize_w(0, a)
+        gather_words(2, 0, 1)
+        gather_words(2, 1, 2)
+        read_tile(0, 0)
+        read_tile(0, 1)
+        cast_w(1, 0)
+        cast_w(1, 1, on="codes0_2")
+        cast_w(1, 2, on="w_raw1_1_0")
+        cast_w(2, 0, on="w_raw1_2_0")
+
+        pick_second(0, 0, 0, NCMP)
+        subtract(0, 0, 0, NCMP)
+        quantize_w(1, 0, on="scales0_2")
+        floor_and_move(0, 0)
+        quantize_w(1, 1)
+        quantize_w(1, 2)
+        read_tile(1, 0, on="w_raw2_0_0")
+        cast_w(2, 1)
+        read_tile(1, 1, on="w_raw2_1_0")
+        cast_w(2, 2, on="w_raw2_1_0", skip=4096)
+
+        pick_second(0, 1, 0, NCMP, on="wb1_2")
+        subtract(0, 1, 0, NCMP)
+        quantize_w(2, 0)
+        pick_second(1, 0, 0, NCMP, on="wb2_0")
+        floor_and_move(0, 1)
+        subtract(1, 0, 0, NCMP)
+        quantize_w(2, 1)
+        pick_second(1, 1, 0, NCMP, on="wb2_1")
+        floor_and_move(1, 0)
+        subtract(1, 1, 0, NCMP)
+        quantize_w(2, 2)
+        floor_and_move(1, 1, on="wb2_2")
+        for u in range(4):
+            read_tile(2, u)
+        woven0 = weave(z0[:], NCMP, nc.scalar.copy, "woven0", on="codes2_2")
+
+        out_rows = out.rearrange("(i p) j -> p i j", p=P)
+        quantized = {}
+
+        def second_product(j0, j1):
+            width = j1 - j0
+            accs = [psum.tile([P, width], F32, name="acc2", tag=f"bank{i}") for i in range(N // P)]
+            steps = [(i, c) for i in range(N // P) for c in range(0, width, P)]
+            for b, base in ((0, j0), (1, 0)):
+                zc, zs = quantized[b, j0 * b]
+                for i, c in steps:
+                    nc.tensor.matmul_mx(
+                        out=accs[i][:, c : c + P],
+                        lhsT=w4[:, b, 2 * P * i : 2 * P * (i + 1)].bitcast(FP4X4),
+                        lhsT_scale=w4_sc[:, b, P * i : P * (i + 1)],
+                        rhs=zc[:, base + c : base + c + P].bitcast(FP8X4),
+                        rhs_scale=zs[:, base + c : base + c + P],
+                        start=(b == 0 and c == 0),
+                        stop=(b == 1 and c == width - P),
+                    )
+            for half in range(2):
+                res = held([P, 3, width], F32, f"res{j0}_{half}")
+                for k in range(3):
+                    if half == 1 and j0 > 0:
+                        nc.vector.tensor_copy(out=res[:, k, :], in_=accs[3 * half + k][:])
+                    else:
+                        nc.scalar.copy(out=res[:, k, :], in_=accs[3 * half + k][:])
+                queue = nc.scalar if (half == 0 and j0 > 0) else nc.sync
+                queue.dma_start(out=out_rows[:, 3 * half : 3 * half + 3, j0:j1], in_=res[:])
+
+        chunks = ((0, HEAD_COLS), (HEAD_COLS, NCMP))
+        z1 = {j0: held([P, 4, j1 - j0], BF16, f"z_high{j0}") for j0, j1 in chunks}
+        units = [(u, j0, j1) for j0, j1 in chunks for u in range(4)]
+        pick_second(2, 0, 0, HEAD_COLS)
+        for n, (u, j0, j1) in enumerate(units):
+            subtract(2, u, j0, j1)
+            if n + 1 < len(units):
+                on = None
+                if n + 1 == 3:
+                    quantized[0, 0] = quantize_z(woven0, NCMP, "0")
+                    on = "woven0"
+                if n + 1 == 7:
+                    quantized[1, 0] = quantize_z(woven_head, HEAD_COLS, "1_0")
+                    on = "woven_head"
+                pick_second(2, units[n + 1][0], units[n + 1][1], units[n + 1][2], on=on)
+            floor(2, u, j0, j1, z1[j0][:, u, :])
+            if n == 3:
+                woven_head = weave(z1[0][:], HEAD_COLS, nc.scalar.copy, "woven_head")
+            if n == 6:
+                second_product(0, HEAD_COLS)
+        woven_tail = weave(z1[HEAD_COLS][:], NCMP - HEAD_COLS, nc.vector.tensor_copy, "woven_tail")
+        quantized[1, HEAD_COLS] = quantize_z(woven_tail, NCMP - HEAD_COLS, "1_tail")
+        second_product(HEAD_COLS, NCMP)
+
+
+def math_size(shape, dtype):
+    count = 1
+    for n in shape[1:]:
+        count = count * n
+    return count * {F32: 4, U32: 4, BF16: 2, U16: 2, U8: 1}[dtype]

@@ -47,12 +47,17 @@ def tile_list_punch_station_margins_kernel(
             places[name] = (start, space if skip or on is None else space)
             return keep.tile(shape, dtype, name=name, offset=start, align_bytes=64)
 
+        def region(name, size):
+            places[name] = (used[0], size)
+            used[0] = used[0] + size
+
         offs_t = lists.tile([P, S // 16], U16, name="offs_t")
         pos1_t = lists.tile([P, NCMP // 16], U16, name="pos1_t")
         pos2_t = lists.tile([P, NCMP // 16], U16, name="pos2_t")
 
-        tab = [held([P, T], U16, f"tab{a}") for a in range(PASSES)]
-        tab_sc = held([P, T], U8, "tab_sc")
+        tab = [held([P, T], U16, f"tab{a}", room=8192 + 1792) for a in range(PASSES)]
+        region("scale_rows", 2560 + 4096)
+        tab_sc = held([P, T], U8, "tab_sc", on="scale_rows", skip=2560)
         nc.vector.memset(tab_sc[:].bitcast(I32), 0)
         for q in range(4):
             nc.gpsimd.dma_start(
@@ -66,29 +71,23 @@ def tile_list_punch_station_margins_kernel(
         planes = [held([P, S], U8, f"plane{a}") for a in range(PASSES)]
         for a in range(1, PASSES):
             nc.vector.memset(planes[a][:].bitcast(I32), 0)
-        w4_sc = held([P, 2, N], U8, "w4_sc")
-        nc.vector.memset(w4_sc[:].rearrange("p a n -> p (a n)").bitcast(I32), 0)
 
         w_raw = {}
 
         def load_tab(a):
             nc.sync.dma_start(out=tab[a][:].bitcast(I32), in_=tab_words[a].bitcast(I32))
 
-        def load_w(g, a, parts=1):
+        def load_w(g, a, on=None, skip=0):
             c0, nt = GROUPS[g]
-            width = nt * P // parts
-            w_raw[g, a] = []
-            for k in range(parts):
-                raw = held([P, 4, width], F32, f"w_raw{g}_{a}_{k}")
-                rows = w1[512 * a : 512 * (a + 1), c0 + k * width : c0 + (k + 1) * width]
-                nc.sync.dma_start(out=raw[:], in_=rows.rearrange("(p j) c -> p j c", j=4))
-                w_raw[g, a].append(raw)
+            w_raw[g, a] = held([P, 4, nt * P], F32, f"w_raw{g}_{a}", on=on, skip=skip)
+            rows = w1[512 * a : 512 * (a + 1), c0 : c0 + nt * P]
+            nc.sync.dma_start(out=w_raw[g, a][:], in_=rows.rearrange("(p j) c -> p j c", j=4))
 
         marg = {}
 
-        def load_margin(g):
+        def load_margin(g, on, skip=0):
             c0, nt = GROUPS[g]
-            marg[g] = held([P, nt, NCMP], F32, f"marg{g}")
+            marg[g] = held([P, nt, NCMP], F32, f"marg{g}", on=on, skip=skip)
             nc.sync.dma_start(out=marg[g][:], in_=margin[c0 : c0 + nt * P, :].rearrange("(p u) j -> p u j", u=nt))
 
         nc.sync.dma_start(offs_t[:], offs)
@@ -98,34 +97,16 @@ def tile_list_punch_station_margins_kernel(
         load_w(0, 1)
         load_w(0, 2)
         load_tab(2)
-        load_w(1, 0)
         nc.sync.dma_start(pos2_t[:], pos2)
         nc.sync.dma_start(pos1_t[:], pos1)
         gain_low = held([P, 2, 2], F32, "gain_low")
         nc.sync.dma_start(out=gain_low[:], in_=gain[0:512].rearrange("(g p u) -> p g u", g=2, u=2))
-        load_w(1, 1)
-        load_margin(0)
-        load_w(1, 2)
-        load_w(2, 0)
-        load_w(2, 1)
-        load_margin(1)
-        load_w(2, 2, 2)
-        gain_high = held([P, 4], F32, "gain_high")
-        nc.sync.dma_start(out=gain_high[:], in_=gain[512:1024].rearrange("(p u) -> p u", u=4))
-        gains = [gain_low[:, 0, :], gain_low[:, 1, :], gain_high[:]]
-        load_margin(2)
-        w4 = held([P, 2, 2 * N], U8, "w4")
-        nc.sync.dma_start(out=w4[:].bitcast(I32), in_=w4_words.bitcast(I32).rearrange("a p c -> p a c"))
-        for q in range(4):
-            nc.sync.dma_start(
-                out=w4_sc[32 * q : 32 * q + 4].bitcast(I32),
-                in_=w4_scales[:, 4 * q : 4 * q + 4, :].bitcast(I32).rearrange("a r c -> r a c"),
-            )
+        gains = [gain_low[:, 0, :], gain_low[:, 1, :]]
 
         v = {}
 
-        def gather_words(a, s0, s1, on=None):
-            got = held([P, (s1 - s0) * BANK], U16, f"v{a}_{s0}", on=on)
+        def gather_words(a, s0, s1, on=None, skip=0):
+            got = held([P, (s1 - s0) * BANK], U16, f"v{a}_{s0}", on=on, skip=skip)
             nc.vector.tensor_copy(out=got[:], in_=tab[a][:].indirect(offs_t[:, 32 * s0 : 32 * s1]))
             for s in range(s0, s1):
                 v[a, s] = got[:, (s - s0) * BANK : (s - s0 + 1) * BANK]
@@ -134,20 +115,18 @@ def tile_list_punch_station_margins_kernel(
 
         def cast_w(g, a, on=None, skip=0):
             nt = GROUPS[g][1]
-            wb[g, a] = held([P, nt * 512], BF16, f"wb{g}_{a}", on=on, skip=skip)
+            wb[g, a] = held([P, nt * 512], BF16, f"wb{g}_{a}", room=4096, on=on, skip=skip)
             if nt == 2:
                 dst = wb[g, a][:].rearrange("p (u m e j) -> p m j e u", u=2, e=2, j=4)
-                nc.scalar.copy(out=dst, in_=w_raw[g, a][0][:].rearrange("p j (m e u) -> p m j e u", e=2, u=2))
+                nc.scalar.copy(out=dst, in_=w_raw[g, a][:].rearrange("p j (m e u) -> p m j e u", e=2, u=2))
             else:
                 dst = wb[g, a][:].rearrange("p (u m j) -> p m j u", u=4, j=4)
-                rows = P // len(w_raw[g, a])
-                for k, raw in enumerate(w_raw[g, a]):
-                    nc.scalar.copy(out=dst[:, k * rows : (k + 1) * rows], in_=raw[:].rearrange("p j (m u) -> p m j u", u=4))
+                nc.scalar.copy(out=dst, in_=w_raw[g, a][:].rearrange("p j (m u) -> p m j u", u=4))
 
-        def quantize_w(g, a, on=None):
+        def quantize_w(g, a, scales_on=None, scales_skip=0, codes_on=None, codes_skip=0):
             nt = GROUPS[g][1]
-            codes[g, a] = held([P, nt * P], U32, f"codes{g}_{a}", room=4096, on=on)
-            scales[g, a] = held([P, nt * P], U8, f"scales{g}_{a}", room=1024)
+            codes[g, a] = held([P, nt * P], U32, f"codes{g}_{a}", on=codes_on, skip=codes_skip)
+            scales[g, a] = held([P, nt * P], U8, f"scales{g}_{a}", on=scales_on, skip=scales_skip)
             nc.vector.quantize_mx(out=codes[g, a][:].bitcast(FP8X4), scales=scales[g, a][:], in_=wb[g, a][:])
 
         banks = [0]
@@ -173,11 +152,11 @@ def tile_list_punch_station_margins_kernel(
         second, diff = {}, {}
 
         def pick_second(g, u, j0, j1, on=None):
-            second[g, u, j0] = held([P, j1 - j0], F32, f"second{g}_{u}_{j0}", on=on)
+            second[g, u, j0] = held([P, j1 - j0], F32, f"second{g}_{u}_{j0}", room=4096 if (g, u) == (0, 0) else 0, on=on)
             nc.vector.tensor_copy(out=second[g, u, j0][:], in_=hs[g, u][:].indirect(pos2_t[:, j0 // 16 : j1 // 16]))
 
-        def subtract(g, u, j0, j1):
-            diff[g, u, j0] = held([P, j1 - j0], F32, f"diff{g}_{u}_{j0}")
+        def subtract(g, u, j0, j1, on=None):
+            diff[g, u, j0] = held([P, j1 - j0], F32, f"diff{g}_{u}_{j0}", room=8192 if g == 0 else (3072 if g == 1 else 0), on=on)
             nc.vector.tensor_tensor(
                 diff[g, u, j0][:], hs[g, u][:].indirect(pos1_t[:, j0 // 16 : j1 // 16]), second[g, u, j0][:], ALU.subtract
             )
@@ -220,53 +199,77 @@ def tile_list_punch_station_margins_kernel(
             z = held([P, NCMP], BF16, f"z{g}_{u}", on=on)
             floor(g, u, 0, NCMP, z[:])
             for e in range(2):
-                nc.gpsimd.dma_start(out=z0[64 * g : 64 * g + 64, 2 * e + u, :], in_=z[e:P:2, :])
+                nc.sync.dma_start(out=z0[64 * g : 64 * g + 64, 2 * e + u, :], in_=z[e:P:2, :])
 
         gather_words(0, 0, 2)
         nc.vector.tensor_copy(out=planes[0][:], in_=tab_sc[:].indirect(offs_t[:]))
         for a in range(1, PASSES):
-            nc.gpsimd.dma_start(
+            nc.sync.dma_start(
                 out=planes[a][0:MOVED_ROWS, :].bitcast(I32),
                 in_=planes[0][4 * a : 4 * a + MOVED_ROWS, :].bitcast(I32),
             )
+        load_w(1, 0, "scale_rows")
         cast_w(0, 0)
         quantize_w(0, 0)
-        gather_words(1, 0, 2, on="tab_sc")
-        for a in (1, 2):
-            cast_w(0, a)
-            quantize_w(0, a)
-        gather_words(2, 0, 1)
-        gather_words(2, 1, 2)
+        gather_words(1, 0, 2, "tab_sc", 2048)
+        load_w(1, 1, "tab1")
+        load_margin(0, "tab1", 4096)
+        cast_w(0, 1)
+        quantize_w(0, 1, "tab_sc", 1536)
+        cast_w(0, 2)
+        region("last_codes", 2048 + 8192)
+        quantize_w(0, 2, "tab_sc", 1792, "last_codes", 1536)
+        load_w(1, 2, "wb0_2")
+        gather_words(2, 0, 1, "wb0_1")
+        gather_words(2, 1, 2, "wb0_1", 1024)
+        load_w(2, 0, "tab2", 1792)
         read_tile(0, 0)
         read_tile(0, 1)
+        load_w(2, 1, "last_codes", 2048)
         cast_w(1, 0)
-        cast_w(1, 1, on="codes0_2")
-        cast_w(1, 2, on="w_raw1_1_0")
-        cast_w(2, 0, on="w_raw1_2_0")
+        quantize_w(1, 0, "tab2")
+        w4_sc = held([P, 2, N], U8, "w4_sc", on="tab2", skip=256)
+        nc.vector.memset(w4_sc[:].rearrange("p a n -> p (a n)").bitcast(I32), 0)
+        for q in range(4):
+            nc.sync.dma_start(
+                out=w4_sc[32 * q : 32 * q + 4].bitcast(I32),
+                in_=w4_scales[:, 4 * q : 4 * q + 4, :].bitcast(I32).rearrange("a r c -> r a c"),
+            )
+        cast_w(1, 1, "last_codes")
+        cast_w(1, 2, "w_raw1_1")
+        cast_w(2, 0, "w_raw1_2")
 
         pick_second(0, 0, 0, NCMP)
         subtract(0, 0, 0, NCMP)
-        quantize_w(1, 0, on="scales0_2")
+        load_margin(1, "second0_0_0")
         floor_and_move(0, 0)
+        load_w(2, 2, "diff0_0_0")
         quantize_w(1, 1)
         quantize_w(1, 2)
-        read_tile(1, 0, on="w_raw2_0_0")
+        read_tile(1, 0, on="w_raw2_0")
         cast_w(2, 1)
-        read_tile(1, 1, on="w_raw2_1_0")
-        cast_w(2, 2, on="w_raw2_1_0", skip=4096)
+        read_tile(1, 1, on="w_raw2_1")
+        cast_w(2, 2, "w_raw2_1", 4096)
 
         pick_second(0, 1, 0, NCMP, on="wb1_2")
         subtract(0, 1, 0, NCMP)
         quantize_w(2, 0)
         pick_second(1, 0, 0, NCMP, on="wb2_0")
         floor_and_move(0, 1)
+        load_margin(2, "diff0_1_0")
         subtract(1, 0, 0, NCMP)
+        gain_high = held([P, 4], F32, "gain_high", on="second1_0_0")
+        nc.sync.dma_start(out=gain_high[:], in_=gain[512:1024].rearrange("(p u) -> p u", u=4))
+        gains.append(gain_high[:])
         quantize_w(2, 1)
         pick_second(1, 1, 0, NCMP, on="wb2_1")
         floor_and_move(1, 0)
-        subtract(1, 1, 0, NCMP)
-        quantize_w(2, 2)
-        floor_and_move(1, 1, on="wb2_2")
+        w4 = held([P, 2, 2 * N], U8, "w4", on="diff1_0_0")
+        nc.sync.dma_start(out=w4[:].bitcast(I32), in_=w4_words.bitcast(I32).rearrange("a p c -> p a c"))
+        region("last_codes_high", 4096)
+        quantize_w(2, 2, codes_on="last_codes_high")
+        subtract(1, 1, 0, NCMP, on="wb2_2")
+        floor_and_move(1, 1)
         for u in range(4):
             read_tile(2, u)
         woven0 = weave(z0[:], NCMP, nc.scalar.copy, "woven0", on="codes2_2")

@@ -15,13 +15,20 @@ FP8X4 = mybir.dt.float8_e4m3fn_x4
 FP4X4 = mybir.dt.float4_e2m1fn_x4
 ALU = mybir.AluOpType
 TANH = mybir.ActivationFunctionType.Tanh
+BYTES_OF = {F32: 4, U32: 4, BF16: 2, U16: 2, U8: 1}
 
 P = 128
-PASSES = K // 512
+PACK = 4
+K_PASS = P * PACK
+PASSES = K // K_PASS
 BANK = 512
-HEAD_COLS = 384
-MOVED_ROWS = 112
+BANKS = 8
+LIST_ROWS = 16
+ALIGN = 64
+KB = 1024
 GROUPS = ((0, 2), (256, 2), (512, 4))
+MOVED_ROWS = 112
+HEAD_COLS = 384
 
 
 def tile_list_punch_station_margins_kernel(
@@ -36,132 +43,133 @@ def tile_list_punch_station_margins_kernel(
         places = {}
         used = [0]
 
-        def held(shape, dtype, name, room=0, on=None, skip=0):
-            size = math_size(shape, dtype)
-            if on is None:
-                start, space = used[0], max(size, room)
-                used[0] = start + (space + 63) // 64 * 64
-            else:
-                start, space = places[on][0] + skip, places[on][1] - skip
-                assert size <= space, name
-            places[name] = (start, space if skip or on is None else space)
-            return keep.tile(shape, dtype, name=name, offset=start, align_bytes=64)
-
         def region(name, size):
             places[name] = (used[0], size)
-            used[0] = used[0] + size
+            used[0] = used[0] + (size + ALIGN - 1) // ALIGN * ALIGN
 
-        offs_t = lists.tile([P, S // 16], U16, name="offs_t")
-        pos1_t = lists.tile([P, NCMP // 16], U16, name="pos1_t")
-        pos2_t = lists.tile([P, NCMP // 16], U16, name="pos2_t")
+        def held(shape, dtype, name, room=0, on=None, skip=0):
+            size = BYTES_OF[dtype]
+            for extent in shape[1:]:
+                size = size * extent
+            if on is None:
+                region(name, max(size, room))
+            else:
+                places[name] = (places[on][0] + skip, places[on][1] - skip)
+            assert size <= places[name][1], name
+            return keep.tile(shape, dtype, name=name, offset=places[name][0], align_bytes=ALIGN)
 
-        tab = [held([P, T], U16, f"tab{a}", room=8192 + 1792) for a in range(PASSES)]
-        region("scale_rows", 2560 + 4096)
+        offs_t = lists.tile([P, S // LIST_ROWS], U16, name="offs_t")
+        pos1_t = lists.tile([P, NCMP // LIST_ROWS], U16, name="pos1_t")
+        pos2_t = lists.tile([P, NCMP // LIST_ROWS], U16, name="pos2_t")
+
+        region("later_words", 1 * KB + 3840 + 4 * KB + 8 * KB)
+        tab = [held([P, T], U16, "tab0"), held([P, T], U16, "tab1", on="later_words")]
+
+        region("scale_rows", 2560 + T)
         tab_sc = held([P, T], U8, "tab_sc", on="scale_rows", skip=2560)
         nc.vector.memset(tab_sc[:].bitcast(I32), 0)
         for q in range(4):
-            nc.gpsimd.dma_start(
+            (nc.gpsimd if q < 2 else nc.scalar).dma_start(
                 out=tab_sc[32 * q : 32 * q + 4 * PASSES, :].bitcast(I32),
                 in_=tab_scales[:, 4 * q : 4 * q + 4, :].bitcast(I32),
             )
-        warm = held([P, 8], F32, "warm")
-        nc.vector.memset(warm[:], 0.0)
-        warm_out = held([P, 8], F32, "warm_out")
-        nc.scalar.activation(out=warm_out[:], in_=warm[:], func=TANH)
-        planes = [held([P, S], U8, f"plane{a}") for a in range(PASSES)]
+        planes = {a: held([P, S], U8, f"plane{a}") for a in range(1, PASSES)}
         for a in range(1, PASSES):
             nc.vector.memset(planes[a][:].bitcast(I32), 0)
 
-        w_raw = {}
+        w_raw, marg = {}, {}
 
         def load_tab(a):
             nc.sync.dma_start(out=tab[a][:].bitcast(I32), in_=tab_words[a].bitcast(I32))
 
         def load_w(g, a, on=None, skip=0):
             c0, nt = GROUPS[g]
-            w_raw[g, a] = held([P, 4, nt * P], F32, f"w_raw{g}_{a}", on=on, skip=skip)
-            rows = w1[512 * a : 512 * (a + 1), c0 : c0 + nt * P]
-            nc.sync.dma_start(out=w_raw[g, a][:], in_=rows.rearrange("(p j) c -> p j c", j=4))
+            w_raw[g, a] = held([P, PACK, nt * P], F32, f"w_raw{g}_{a}", on=on, skip=skip)
+            rows = w1[K_PASS * a : K_PASS * (a + 1), c0 : c0 + nt * P]
+            nc.sync.dma_start(out=w_raw[g, a][:], in_=rows.rearrange("(p i) c -> p i c", i=PACK))
 
-        marg = {}
-
-        def load_margin(g, on, skip=0):
+        def load_margin(g, on):
             c0, nt = GROUPS[g]
-            marg[g] = held([P, nt, NCMP], F32, f"marg{g}", on=on, skip=skip)
+            marg[g] = held([P, nt, NCMP], F32, f"marg{g}", on=on)
             nc.sync.dma_start(out=marg[g][:], in_=margin[c0 : c0 + nt * P, :].rearrange("(p u) j -> p u j", u=nt))
 
         nc.sync.dma_start(offs_t[:], offs)
         load_tab(0)
-        load_w(0, 0)
         load_tab(1)
-        load_w(0, 1)
-        load_w(0, 2)
-        load_tab(2)
+        load_w(0, 0)
         nc.sync.dma_start(pos2_t[:], pos2)
         nc.sync.dma_start(pos1_t[:], pos1)
         gain_low = held([P, 2, 2], F32, "gain_low")
-        nc.sync.dma_start(out=gain_low[:], in_=gain[0:512].rearrange("(g p u) -> p g u", g=2, u=2))
+        nc.sync.dma_start(out=gain_low[:], in_=gain[0:K_PASS].rearrange("(g p u) -> p g u", g=2, u=2))
         gains = [gain_low[:, 0, :], gain_low[:, 1, :]]
 
-        v = {}
+        picked = {}
 
         def gather_words(a, s0, s1, on=None, skip=0):
-            got = held([P, (s1 - s0) * BANK], U16, f"v{a}_{s0}", on=on, skip=skip)
-            nc.vector.tensor_copy(out=got[:], in_=tab[a][:].indirect(offs_t[:, 32 * s0 : 32 * s1]))
+            got = held([P, (s1 - s0) * BANK], U16, f"picked{a}_{s0}", on=on, skip=skip)
+            entries = offs_t[:, s0 * BANK // LIST_ROWS : s1 * BANK // LIST_ROWS]
+            nc.vector.tensor_copy(out=got[:], in_=tab[a][:].indirect(entries))
             for s in range(s0, s1):
-                v[a, s] = got[:, (s - s0) * BANK : (s - s0 + 1) * BANK]
+                picked[a, s] = got[:, (s - s0) * BANK : (s - s0 + 1) * BANK]
 
         wb, codes, scales = {}, {}, {}
 
-        def cast_w(g, a, on=None, skip=0):
+        def cast_w(g, a, u0=0, count=None, room=4 * KB, on=None, skip=0, copy=nc.scalar.copy):
             nt = GROUPS[g][1]
-            wb[g, a] = held([P, nt * 512], BF16, f"wb{g}_{a}", room=4096, on=on, skip=skip)
+            count = count or nt
+            wb[g, a, u0] = held([P, count * K_PASS], BF16, f"wb{g}_{a}_{u0}", room=room, on=on, skip=skip)
             if nt == 2:
-                dst = wb[g, a][:].rearrange("p (u m e j) -> p m j e u", u=2, e=2, j=4)
-                nc.scalar.copy(out=dst, in_=w_raw[g, a][:].rearrange("p j (m e u) -> p m j e u", e=2, u=2))
+                dst = wb[g, a, u0][:].rearrange("p (u m e i) -> p m i e u", u=2, e=2, i=PACK)
+                src = w_raw[g, a][:].rearrange("p i (m e u) -> p m i e u", e=2, u=2)
             else:
-                dst = wb[g, a][:].rearrange("p (u m j) -> p m j u", u=4, j=4)
-                nc.scalar.copy(out=dst, in_=w_raw[g, a][:].rearrange("p j (m u) -> p m j u", u=4))
+                dst = wb[g, a, u0][:].rearrange("p (u m i) -> p m i u", u=count, i=PACK)
+                src = w_raw[g, a][:].rearrange("p i (m u) -> p m i u", u=nt)[:, :, :, u0 : u0 + count]
+            copy(out=dst, in_=src)
 
-        def quantize_w(g, a, scales_on=None, scales_skip=0, codes_on=None, codes_skip=0):
-            nt = GROUPS[g][1]
-            codes[g, a] = held([P, nt * P], U32, f"codes{g}_{a}", on=codes_on, skip=codes_skip)
-            scales[g, a] = held([P, nt * P], U8, f"scales{g}_{a}", on=scales_on, skip=scales_skip)
-            nc.vector.quantize_mx(out=codes[g, a][:].bitcast(FP8X4), scales=scales[g, a][:], in_=wb[g, a][:])
+        def quantize_w(g, a, u0=0, scales_on=None, scales_skip=0, codes_on=None, codes_skip=0):
+            width = wb[g, a, u0].shape[1] // PACK
+            made = held([P, width], U32, f"codes{g}_{a}_{u0}", room=3 * KB, on=codes_on, skip=codes_skip)
+            plane = held([P, width], U8, f"scales{g}_{a}_{u0}", on=scales_on, skip=scales_skip)
+            nc.vector.quantize_mx(out=made[:].bitcast(FP8X4), scales=plane[:], in_=wb[g, a, u0][:])
+            for k in range(width // P):
+                codes[g, a, u0 + k] = made[:, k * P : (k + 1) * P]
+                scales[g, a, u0 + k] = plane[:, k * P : (k + 1) * P]
 
-        banks = [0]
-        hs = {}
+        banks_taken = [0]
+        reading = {}
 
         def read_tile(g, u, on=None):
-            hs[g, u] = held([P, S], F32, f"h{g}_{u}", on=on)
-            for s in range(2):
-                acc = psum.tile([P, BANK], F32, name="acc", tag=f"bank{banks[0] % 8}")
-                banks[0] = banks[0] + 1
+            reading[g, u] = held([P, S], F32, f"reading{g}_{u}", on=on)
+            for s in range(S // BANK):
+                acc = psum.tile([P, BANK], F32, name="acc", tag=f"bank{banks_taken[0] % BANKS}")
+                banks_taken[0] = banks_taken[0] + 1
                 for a in range(PASSES):
                     nc.tensor.matmul_mx(
                         out=acc[:],
-                        lhsT=codes[g, a][:, u * P : (u + 1) * P].bitcast(FP8X4),
-                        lhsT_scale=scales[g, a][:, u * P : (u + 1) * P],
-                        rhs=v[a, s].bitcast(FP4X4),
+                        lhsT=codes[g, a, u].bitcast(FP8X4),
+                        lhsT_scale=scales[g, a, u],
+                        rhs=picked[a, s].bitcast(FP4X4),
                         rhs_scale=planes[a][:, s * BANK : (s + 1) * BANK],
                         start=(a == 0),
                         stop=(a == PASSES - 1),
                     )
-                nc.scalar.activation(out=hs[g, u][:, s * BANK : (s + 1) * BANK], in_=acc[:], func=TANH)
+                nc.scalar.activation(out=reading[g, u][:, s * BANK : (s + 1) * BANK], in_=acc[:], func=TANH)
 
-        second, diff = {}, {}
+        neighbour, diff = {}, {}
 
-        def pick_second(g, u, j0, j1, on=None):
-            second[g, u, j0] = held([P, j1 - j0], F32, f"second{g}_{u}_{j0}", room=4096 if (g, u) == (0, 0) else 0, on=on)
-            nc.vector.tensor_copy(out=second[g, u, j0][:], in_=hs[g, u][:].indirect(pos2_t[:, j0 // 16 : j1 // 16]))
+        def pick_neighbour(g, u, j0=0, j1=NCMP, on=None, skip=0):
+            neighbour[g, u, j0] = held([P, j1 - j0], F32, f"neighbour{g}_{u}_{j0}", on=on, skip=skip)
+            entries = pos2_t[:, j0 // LIST_ROWS : j1 // LIST_ROWS]
+            nc.vector.tensor_copy(out=neighbour[g, u, j0][:], in_=reading[g, u][:].indirect(entries))
 
-        def subtract(g, u, j0, j1, on=None):
-            diff[g, u, j0] = held([P, j1 - j0], F32, f"diff{g}_{u}_{j0}", room=8192 if g == 0 else (3072 if g == 1 else 0), on=on)
+        def subtract(g, u, j0=0, j1=NCMP, room=0, on=None, skip=0):
+            diff[g, u, j0] = held([P, j1 - j0], F32, f"diff{g}_{u}_{j0}", room=room, on=on, skip=skip)
+            entries = pos1_t[:, j0 // LIST_ROWS : j1 // LIST_ROWS]
             nc.vector.tensor_tensor(
-                diff[g, u, j0][:], hs[g, u][:].indirect(pos1_t[:, j0 // 16 : j1 // 16]), second[g, u, j0][:], ALU.subtract
+                diff[g, u, j0][:], reading[g, u][:].indirect(entries), neighbour[g, u, j0][:], ALU.subtract
             )
 
-        def floor(g, u, j0, j1, z):
+        def hold_above_margin(g, u, j0, j1, z):
             nc.vector.scalar_tensor_tensor(
                 out=z,
                 in0=diff[g, u, j0][:],
@@ -171,165 +179,173 @@ def tile_list_punch_station_margins_kernel(
                 op1=ALU.max,
             )
 
-        def weave(z, width, engine_copy, name, on=None):
-            woven = held([P, 4 * width], BF16, name, on=on)
-            engine_copy(
-                out=woven[:].rearrange("p (c i t) -> p c t i", i=4, t=4),
-                in_=z.rearrange("p t (c i) -> p c t i", i=4),
+        def weave(z, width, copy, name, on=None):
+            woven = held([P, PACK * width], BF16, name, on=on)
+            copy(
+                out=woven[:].rearrange("p (c e t) -> p c t e", e=4, t=PACK),
+                in_=z.rearrange("p t (c e) -> p c t e", e=4),
             )
             return woven
 
-        def quantize_z(woven, width, name):
-            zc = held([P, width], U32, f"zc{name}")
-            zs = held([P, width], U8, f"zs{name}")
+        def quantize_z(woven, widths, name):
+            z_codes = held([P, sum(widths)], U32, f"z_codes_{name}")
+            z_scales = held([P, sum(widths)], U8, f"z_scales_{name}")
             c0 = 0
-            while c0 < width:
-                step = 512 if width - c0 >= 512 else (256 if width - c0 >= 256 else 128)
+            for width in widths:
                 nc.vector.quantize_mx(
-                    out=zc[:, c0 : c0 + step].bitcast(FP8X4),
-                    scales=zs[:, c0 : c0 + step],
-                    in_=woven[:, 4 * c0 : 4 * (c0 + step)],
+                    out=z_codes[:, c0 : c0 + width].bitcast(FP8X4),
+                    scales=z_scales[:, c0 : c0 + width],
+                    in_=woven[:, PACK * c0 : PACK * (c0 + width)],
                 )
-                c0 = c0 + step
-            return zc, zs
+                c0 = c0 + width
+            return z_codes, z_scales
 
-        z0 = held([P, 4, NCMP], BF16, "z0")
+        z_low = held([P, PACK, NCMP], BF16, "z_low")
 
-        def floor_and_move(g, u, on=None):
-            z = held([P, NCMP], BF16, f"z{g}_{u}", on=on)
-            floor(g, u, 0, NCMP, z[:])
+        def finish_low_tile(g, u, on=None, skip=0):
+            z = held([P, NCMP], BF16, f"z{g}_{u}", on=on, skip=skip)
+            hold_above_margin(g, u, 0, NCMP, z[:])
             for e in range(2):
-                nc.sync.dma_start(out=z0[64 * g : 64 * g + 64, 2 * e + u, :], in_=z[e:P:2, :])
+                nc.sync.dma_start(out=z_low[64 * g : 64 * g + 64, 2 * e + u, :], in_=z[e:P:2, :])
 
         gather_words(0, 0, 2)
+        load_w(0, 1, on="tab0")
+        load_w(0, 2, on="tab0", skip=4 * KB)
+        gather_words(1, 0, 2)
+        tab.append(held([P, T], U16, "tab2", on="later_words", skip=1 * KB))
+        load_tab(2)
+        planes[0] = held([P, S], U8, "plane0", on="later_words")
         nc.vector.tensor_copy(out=planes[0][:], in_=tab_sc[:].indirect(offs_t[:]))
         for a in range(1, PASSES):
             nc.sync.dma_start(
                 out=planes[a][0:MOVED_ROWS, :].bitcast(I32),
                 in_=planes[0][4 * a : 4 * a + MOVED_ROWS, :].bitcast(I32),
             )
-        load_w(1, 0, "scale_rows")
-        cast_w(0, 0)
-        quantize_w(0, 0)
-        gather_words(1, 0, 2, "tab_sc", 2048)
-        load_w(1, 1, "tab1")
-        load_margin(0, "tab1", 4096)
+        load_w(1, 0, on="scale_rows")
+        cast_w(0, 0, room=8 * KB)
+        quantize_w(0, 0, scales_on="tab_sc", scales_skip=1536)
+        load_w(1, 1, on="wb0_0_0")
         cast_w(0, 1)
-        quantize_w(0, 1, "tab_sc", 1536)
+        quantize_w(0, 1, scales_on="tab_sc", scales_skip=1536 + 256)
         cast_w(0, 2)
-        region("last_codes", 2048 + 8192)
-        quantize_w(0, 2, "tab_sc", 1792, "last_codes", 1536)
-        load_w(1, 2, "wb0_2")
-        gather_words(2, 0, 1, "wb0_1")
-        gather_words(2, 1, 2, "wb0_1", 1024)
-        load_w(2, 0, "tab2", 1792)
+        region("last_codes", 2 * KB + 8 * KB)
+        quantize_w(0, 2, scales_on="tab_sc", scales_skip=1536 + 512, codes_on="last_codes", codes_skip=1536)
+        load_margin(0, on="wb0_2_0")
+        gather_words(2, 0, 1, on="wb0_1_0")
+        gather_words(2, 1, 2, on="wb0_1_0", skip=1 * KB)
+        load_w(1, 2, on="tab2", skip=3840)
+        load_w(2, 0, on="tab2", skip=3840 + 4 * KB)
         read_tile(0, 0)
         read_tile(0, 1)
-        load_w(2, 1, "last_codes", 2048)
+        load_w(2, 1, on="last_codes", skip=2 * KB)
+
         cast_w(1, 0)
-        quantize_w(1, 0, "tab2")
+        cast_w(1, 1, on="tab2", skip=256 + 1536, copy=nc.vector.tensor_copy)
+        quantize_w(1, 0, scales_on="tab2")
+        quantize_w(1, 1)
         w4_sc = held([P, 2, N], U8, "w4_sc", on="tab2", skip=256)
-        nc.vector.memset(w4_sc[:].rearrange("p a n -> p (a n)").bitcast(I32), 0)
+        nc.vector.memset(w4_sc[:].rearrange("p b n -> p (b n)").bitcast(I32), 0)
         for q in range(4):
             nc.sync.dma_start(
                 out=w4_sc[32 * q : 32 * q + 4].bitcast(I32),
-                in_=w4_scales[:, 4 * q : 4 * q + 4, :].bitcast(I32).rearrange("a r c -> r a c"),
+                in_=w4_scales[:, 4 * q : 4 * q + 4, :].bitcast(I32).rearrange("b r c -> r b c"),
             )
-        cast_w(1, 1, "last_codes")
-        cast_w(1, 2, "w_raw1_1")
-        cast_w(2, 0, "w_raw1_2")
 
-        pick_second(0, 0, 0, NCMP)
-        subtract(0, 0, 0, NCMP)
-        load_margin(1, "second0_0_0")
-        floor_and_move(0, 0)
-        load_w(2, 2, "diff0_0_0")
-        quantize_w(1, 1)
+        cast_w(1, 2, on="last_codes")
+        cast_w(2, 0, on="w_raw1_2")
+
+        pick_neighbour(0, 0, on="w_raw1_1")
+        subtract(0, 0, room=8 * KB)
+        load_w(2, 2, on="neighbour0_0_0")
+        finish_low_tile(0, 0)
+        load_margin(1, on="diff0_0_0")
         quantize_w(1, 2)
         read_tile(1, 0, on="w_raw2_0")
-        cast_w(2, 1)
-        read_tile(1, 1, on="w_raw2_1")
-        cast_w(2, 2, "w_raw2_1", 4096)
+        cast_w(2, 1, u0=0, count=2, on="w_raw2_0", skip=4 * KB)
+        read_tile(1, 1)
+        cast_w(2, 2, u0=0, count=2, on="codes1_2_0")
+        cast_w(2, 1, u0=2, count=2, on="codes1_1_0")
 
-        pick_second(0, 1, 0, NCMP, on="wb1_2")
-        subtract(0, 1, 0, NCMP)
+        pick_neighbour(0, 1, on="wb1_2_0")
+        subtract(0, 1, room=8 * KB)
         quantize_w(2, 0)
-        pick_second(1, 0, 0, NCMP, on="wb2_0")
-        floor_and_move(0, 1)
-        load_margin(2, "diff0_1_0")
-        subtract(1, 0, 0, NCMP)
-        gain_high = held([P, 4], F32, "gain_high", on="second1_0_0")
-        nc.sync.dma_start(out=gain_high[:], in_=gain[512:1024].rearrange("(p u) -> p u", u=4))
+        pick_neighbour(1, 0, on="w_raw2_0", skip=6 * KB)
+        finish_low_tile(0, 1)
+        load_margin(2, on="diff0_1_0")
+        subtract(1, 0, room=3 * KB)
+        gain_high = held([P, PACK], F32, "gain_high", on="neighbour1_0_0")
+        nc.sync.dma_start(out=gain_high[:], in_=gain[K_PASS:H].rearrange("(p u) -> p u", u=PACK))
         gains.append(gain_high[:])
         quantize_w(2, 1)
-        pick_second(1, 1, 0, NCMP, on="wb2_1")
-        floor_and_move(1, 0)
+        pick_neighbour(1, 1, on="wb2_1_0")
+        quantize_w(2, 2)
+        finish_low_tile(1, 0, on="wb2_2_0")
         w4 = held([P, 2, 2 * N], U8, "w4", on="diff1_0_0")
-        nc.sync.dma_start(out=w4[:].bitcast(I32), in_=w4_words.bitcast(I32).rearrange("a p c -> p a c"))
-        region("last_codes_high", 4096)
-        quantize_w(2, 2, codes_on="last_codes_high")
-        subtract(1, 1, 0, NCMP, on="wb2_2")
-        floor_and_move(1, 1)
-        for u in range(4):
-            read_tile(2, u)
-        woven0 = weave(z0[:], NCMP, nc.scalar.copy, "woven0", on="codes2_2")
+        nc.sync.dma_start(out=w4[:].bitcast(I32), in_=w4_words.bitcast(I32).rearrange("b p c -> p b c"))
+        subtract(1, 1, on="wb2_2_0", skip=1 * KB)
+        quantize_w(2, 1, u0=2)
+        finish_low_tile(1, 1, on="w_raw2_1", skip=2 * KB)
+        read_tile(2, 0)
+        read_tile(2, 1)
+        cast_w(2, 2, u0=2, count=2, on="w_raw2_1")
+        pick_neighbour(2, 0, 0, HEAD_COLS)
+        region("last_codes_high", 4 * KB)
+        quantize_w(2, 2, u0=2, codes_on="last_codes_high")
+        read_tile(2, 2)
+        read_tile(2, 3)
+        woven_low = weave(z_low[:], NCMP, nc.scalar.copy, "woven_low", on="last_codes_high")
 
         out_rows = out.rearrange("(i p) j -> p i j", p=P)
-        quantized = {}
+        out_tiles = N // P
+        per_store = out_tiles // 2
 
-        def second_product(j0, j1):
+        def second_product(j0, j1, low, high, stores):
             width = j1 - j0
-            accs = [psum.tile([P, width], F32, name="acc2", tag=f"bank{i}") for i in range(N // P)]
-            steps = [(i, c) for i in range(N // P) for c in range(0, width, P)]
-            for b, base in ((0, j0), (1, 0)):
-                zc, zs = quantized[b, j0 * b]
-                for i, c in steps:
-                    nc.tensor.matmul_mx(
-                        out=accs[i][:, c : c + P],
-                        lhsT=w4[:, b, 2 * P * i : 2 * P * (i + 1)].bitcast(FP4X4),
-                        lhsT_scale=w4_sc[:, b, P * i : P * (i + 1)],
-                        rhs=zc[:, base + c : base + c + P].bitcast(FP8X4),
-                        rhs_scale=zs[:, base + c : base + c + P],
-                        start=(b == 0 and c == 0),
-                        stop=(b == 1 and c == width - P),
-                    )
-            for half in range(2):
-                res = held([P, 3, width], F32, f"res{j0}_{half}")
-                for k in range(3):
-                    if half == 1 and j0 > 0:
-                        nc.vector.tensor_copy(out=res[:, k, :], in_=accs[3 * half + k][:])
-                    else:
-                        nc.scalar.copy(out=res[:, k, :], in_=accs[3 * half + k][:])
-                queue = nc.scalar if (half == 0 and j0 > 0) else nc.sync
-                queue.dma_start(out=out_rows[:, 3 * half : 3 * half + 3, j0:j1], in_=res[:])
+            accs = [psum.tile([P, width], F32, name="acc2", tag=f"bank{i}") for i in range(out_tiles)]
+            for b, (z_codes, z_scales), base in ((0, low, j0), (1, high, 0)):
+                for i in range(out_tiles):
+                    for c in range(0, width, P):
+                        nc.tensor.matmul_mx(
+                            out=accs[i][:, c : c + P],
+                            lhsT=w4[:, b, 2 * P * i : 2 * P * (i + 1)].bitcast(FP4X4),
+                            lhsT_scale=w4_sc[:, b, P * i : P * (i + 1)],
+                            rhs=z_codes[:, base + c : base + c + P].bitcast(FP8X4),
+                            rhs_scale=z_scales[:, base + c : base + c + P],
+                            start=(b == 0 and c == 0),
+                            stop=(b == 1 and c == width - P),
+                        )
+            for half, (copy, queue) in enumerate(stores):
+                res = held([P, per_store, width], F32, f"res{j0}_{half}")
+                for k in range(per_store):
+                    copy(out=res[:, k, :], in_=accs[per_store * half + k][:])
+                queue.dma_start(out=out_rows[:, per_store * half : per_store * (half + 1), j0:j1], in_=res[:])
 
-        chunks = ((0, HEAD_COLS), (HEAD_COLS, NCMP))
-        z1 = {j0: held([P, 4, j1 - j0], BF16, f"z_high{j0}") for j0, j1 in chunks}
-        units = [(u, j0, j1) for j0, j1 in chunks for u in range(4)]
-        pick_second(2, 0, 0, HEAD_COLS)
-        for n, (u, j0, j1) in enumerate(units):
-            subtract(2, u, j0, j1)
-            if n + 1 < len(units):
-                on = None
-                if n + 1 == 3:
-                    quantized[0, 0] = quantize_z(woven0, NCMP, "0")
-                    on = "woven0"
-                if n + 1 == 7:
-                    quantized[1, 0] = quantize_z(woven_head, HEAD_COLS, "1_0")
-                    on = "woven_head"
-                pick_second(2, units[n + 1][0], units[n + 1][1], units[n + 1][2], on=on)
-            floor(2, u, j0, j1, z1[j0][:, u, :])
-            if n == 3:
-                woven_head = weave(z1[0][:], HEAD_COLS, nc.scalar.copy, "woven_head")
-            if n == 6:
-                second_product(0, HEAD_COLS)
-        woven_tail = weave(z1[HEAD_COLS][:], NCMP - HEAD_COLS, nc.vector.tensor_copy, "woven_tail")
-        quantized[1, HEAD_COLS] = quantize_z(woven_tail, NCMP - HEAD_COLS, "1_tail")
-        second_product(HEAD_COLS, NCMP)
+        z_head = held([P, PACK, HEAD_COLS], BF16, "z_head")
+        z_tail = held([P, PACK, NCMP - HEAD_COLS], BF16, "z_tail")
 
+        for u in range(PACK):
+            subtract(2, u, 0, HEAD_COLS)
+            if u == PACK - 2:
+                low = quantize_z(woven_low, (NCMP,), "low")
+            if u < PACK - 1:
+                pick_neighbour(2, u + 1, 0, HEAD_COLS, on={0: "w_raw2_2", PACK - 2: "z_low"}.get(u))
+            else:
+                pick_neighbour(2, 0, HEAD_COLS, NCMP)
+            hold_above_margin(2, u, 0, HEAD_COLS, z_head[:, u, :])
+        woven_head = weave(z_head[:], HEAD_COLS, nc.scalar.copy, "woven_head")
 
-def math_size(shape, dtype):
-    count = 1
-    for n in shape[1:]:
-        count = count * n
-    return count * {F32: 4, U32: 4, BF16: 2, U16: 2, U8: 1}[dtype]
+        for u in range(PACK - 2):
+            subtract(2, u, HEAD_COLS, NCMP)
+            pick_neighbour(2, u + 1, HEAD_COLS, NCMP)
+            hold_above_margin(2, u, HEAD_COLS, NCMP, z_tail[:, u, :])
+        subtract(2, PACK - 2, HEAD_COLS, NCMP)
+        head = quantize_z(woven_head, (256, 128), "head")
+        pick_neighbour(2, PACK - 1, HEAD_COLS, NCMP, on="z_head")
+        hold_above_margin(2, PACK - 2, HEAD_COLS, NCMP, z_tail[:, PACK - 2, :])
+        second_product(0, HEAD_COLS, low, head, ((nc.scalar.copy, nc.sync), (nc.scalar.copy, nc.sync)))
+        subtract(2, PACK - 1, HEAD_COLS, NCMP)
+        hold_above_margin(2, PACK - 1, HEAD_COLS, NCMP, z_tail[:, PACK - 1, :])
+
+        woven_tail = weave(z_tail[:], NCMP - HEAD_COLS, nc.vector.tensor_copy, "woven_tail")
+        tail = quantize_z(woven_tail, (NCMP - HEAD_COLS,), "tail")
+        second_product(HEAD_COLS, NCMP, low, tail, ((nc.scalar.copy, nc.scalar), (nc.vector.tensor_copy, nc.sync)))

from contextlib import ExitStack

import concourse.mybir as mybir

K, T, S, H, NCMP, N = 1536, 4096, 1024, 1024, 512, 768
FLOPS = 2 * K * H * S + 2 * H * N * NCMP

F32 = mybir.dt.float32
BF16 = mybir.dt.bfloat16
I32 = mybir.dt.int32
U32 = mybir.dt.uint32
U16 = mybir.dt.uint16
U8 = mybir.dt.uint8
FP8X4 = mybir.dt.float8_e4m3fn_x4
FP4X4 = mybir.dt.float4_e2m1fn_x4
ALU = mybir.AluOpType
TANH = mybir.ActivationFunctionType.Tanh
BYTES_OF = {F32: 4, U32: 4, BF16: 2, U16: 2, U8: 1}

P = 128
PACK = 4
K_PASS = P * PACK
PASSES = K // K_PASS
BANK = 512
BANKS = 8
LIST_ROWS = 16
ALIGN = 64
KB = 1024
GROUPS = ((0, 2), (256, 2), (512, 4))
MOVED_ROWS = 112
HEAD_COLS = 384


def tile_list_punch_station_margins_kernel(
    tc, tab_words, tab_scales, offs, w1, gain, pos1, pos2, margin, w4_words, w4_scales, out
):
    nc = tc.nc
    with ExitStack() as ctx:
        lists = ctx.enter_context(tc.tile_pool(name="lists", bufs=1))
        keep = ctx.enter_context(tc.tile_pool(name="keep", bufs=1))
        psum = ctx.enter_context(tc.psum_pool(name="psum", bufs=1))

        places = {}
        used = [0]

        def region(name, size):
            places[name] = (used[0], size)
            used[0] = used[0] + (size + ALIGN - 1) // ALIGN * ALIGN

        def held(shape, dtype, name, room=0, on=None, skip=0):
            size = BYTES_OF[dtype]
            for extent in shape[1:]:
                size = size * extent
            if on is None:
                region(name, max(size, room))
            else:
                places[name] = (places[on][0] + skip, places[on][1] - skip)
            assert size <= places[name][1], name
            return keep.tile(shape, dtype, name=name, offset=places[name][0], align_bytes=ALIGN)

        offs_t = lists.tile([P, S // LIST_ROWS], U16, name="offs_t")
        pos1_t = lists.tile([P, NCMP // LIST_ROWS], U16, name="pos1_t")
        pos2_t = lists.tile([P, NCMP // LIST_ROWS], U16, name="pos2_t")

        region("later_words", 1 * KB + 3840 + 4 * KB + 8 * KB)
        tab = [held([P, T], U16, "tab0"), held([P, T], U16, "tab1", on="later_words")]

        region("scale_rows", 2560 + T)
        tab_sc = held([P, T], U8, "tab_sc", on="scale_rows", skip=2560)
        nc.vector.memset(tab_sc[:].bitcast(I32), 0)
        for q in range(4):
            (nc.gpsimd if q < 2 else nc.scalar).dma_start(
                out=tab_sc[32 * q : 32 * q + 4 * PASSES, :].bitcast(I32),
                in_=tab_scales[:, 4 * q : 4 * q + 4, :].bitcast(I32),
            )
        planes = {a: held([P, S], U8, f"plane{a}") for a in range(1, PASSES)}
        for a in range(1, PASSES):
            nc.vector.memset(planes[a][:].bitcast(I32), 0)

        w_raw, marg = {}, {}

        def load_tab(a):
            nc.sync.dma_start(out=tab[a][:].bitcast(I32), in_=tab_words[a].bitcast(I32))

        def load_w(g, a, on=None, skip=0):
            c0, nt = GROUPS[g]
            w_raw[g, a] = held([P, PACK, nt * P], F32, f"w_raw{g}_{a}", on=on, skip=skip)
            rows = w1[K_PASS * a : K_PASS * (a + 1), c0 : c0 + nt * P]
            nc.sync.dma_start(out=w_raw[g, a][:], in_=rows.rearrange("(p i) c -> p i c", i=PACK))

        def load_margin(g, on):
            c0, nt = GROUPS[g]
            marg[g] = held([P, nt, NCMP], F32, f"marg{g}", on=on)
            nc.sync.dma_start(out=marg[g][:], in_=margin[c0 : c0 + nt * P, :].rearrange("(p u) j -> p u j", u=nt))

        nc.sync.dma_start(offs_t[:], offs)
        load_tab(0)
        load_tab(1)
        load_w(0, 0)
        nc.sync.dma_start(pos2_t[:], pos2)
        nc.sync.dma_start(pos1_t[:], pos1)
        gain_low = held([P, 2, 2], F32, "gain_low")
        nc.sync.dma_start(out=gain_low[:], in_=gain[0:K_PASS].rearrange("(g p u) -> p g u", g=2, u=2))
        gains = [gain_low[:, 0, :], gain_low[:, 1, :]]

        picked = {}

        def gather_words(a, s0, s1, on=None, skip=0):
            got = held([P, (s1 - s0) * BANK], U16, f"picked{a}_{s0}", on=on, skip=skip)
            entries = offs_t[:, s0 * BANK // LIST_ROWS : s1 * BANK // LIST_ROWS]
            nc.vector.tensor_copy(out=got[:], in_=tab[a][:].indirect(entries))
            for s in range(s0, s1):
                picked[a, s] = got[:, (s - s0) * BANK : (s - s0 + 1) * BANK]

        wb, codes, scales = {}, {}, {}

        def cast_w(g, a, u0=0, count=None, room=4 * KB, on=None, skip=0, copy=nc.scalar.copy):
            nt = GROUPS[g][1]
            count = count or nt
            wb[g, a, u0] = held([P, count * K_PASS], BF16, f"wb{g}_{a}_{u0}", room=room, on=on, skip=skip)
            if nt == 2:
                dst = wb[g, a, u0][:].rearrange("p (u m e i) -> p m i e u", u=2, e=2, i=PACK)
                src = w_raw[g, a][:].rearrange("p i (m e u) -> p m i e u", e=2, u=2)
            else:
                dst = wb[g, a, u0][:].rearrange("p (u m i) -> p m i u", u=count, i=PACK)
                src = w_raw[g, a][:].rearrange("p i (m u) -> p m i u", u=nt)[:, :, :, u0 : u0 + count]
            copy(out=dst, in_=src)

        def quantize_w(g, a, u0=0, scales_on=None, scales_skip=0, codes_on=None, codes_skip=0):
            width = wb[g, a, u0].shape[1] // PACK
            made = held([P, width], U32, f"codes{g}_{a}_{u0}", room=3 * KB, on=codes_on, skip=codes_skip)
            plane = held([P, width], U8, f"scales{g}_{a}_{u0}", on=scales_on, skip=scales_skip)
            nc.vector.quantize_mx(out=made[:].bitcast(FP8X4), scales=plane[:], in_=wb[g, a, u0][:])
            for k in range(width // P):
                codes[g, a, u0 + k] = made[:, k * P : (k + 1) * P]
                scales[g, a, u0 + k] = plane[:, k * P : (k + 1) * P]

        banks_taken = [0]
        reading = {}

        def read_tile(g, u, on=None):
            reading[g, u] = held([P, S], F32, f"reading{g}_{u}", on=on)
            for s in range(S // BANK):
                acc = psum.tile([P, BANK], F32, name="acc", tag=f"bank{banks_taken[0] % BANKS}")
                banks_taken[0] = banks_taken[0] + 1
                for a in range(PASSES):
                    nc.tensor.matmul_mx(
                        out=acc[:],
                        lhsT=codes[g, a, u].bitcast(FP8X4),
                        lhsT_scale=scales[g, a, u],
                        rhs=picked[a, s].bitcast(FP4X4),
                        rhs_scale=planes[a][:, s * BANK : (s + 1) * BANK],
                        start=(a == 0),
                        stop=(a == PASSES - 1),
                    )
                nc.scalar.activation(out=reading[g, u][:, s * BANK : (s + 1) * BANK], in_=acc[:], func=TANH)

        neighbour, diff = {}, {}

        def pick_neighbour(g, u, j0=0, j1=NCMP, on=None, skip=0):
            neighbour[g, u, j0] = held([P, j1 - j0], F32, f"neighbour{g}_{u}_{j0}", on=on, skip=skip)
            entries = pos2_t[:, j0 // LIST_ROWS : j1 // LIST_ROWS]
            nc.vector.tensor_copy(out=neighbour[g, u, j0][:], in_=reading[g, u][:].indirect(entries))

        def subtract(g, u, j0=0, j1=NCMP, room=0, on=None, skip=0):
            diff[g, u, j0] = held([P, j1 - j0], F32, f"diff{g}_{u}_{j0}", room=room, on=on, skip=skip)
            entries = pos1_t[:, j0 // LIST_ROWS : j1 // LIST_ROWS]
            nc.vector.tensor_tensor(
                diff[g, u, j0][:], reading[g, u][:].indirect(entries), neighbour[g, u, j0][:], ALU.subtract
            )

        def hold_above_margin(g, u, j0, j1, z):
            nc.vector.scalar_tensor_tensor(
                out=z,
                in0=diff[g, u, j0][:],
                scalar=gains[g][:, u : u + 1],
                in1=marg[g][:, u, j0:j1],
                op0=ALU.mult,
                op1=ALU.max,
            )

        def weave(z, width, copy, name, on=None):
            woven = held([P, PACK * width], BF16, name, on=on)
            copy(
                out=woven[:].rearrange("p (c e t) -> p c t e", e=4, t=PACK),
                in_=z.rearrange("p t (c e) -> p c t e", e=4),
            )
            return woven

        def quantize_z(woven, widths, name):
            z_codes = held([P, sum(widths)], U32, f"z_codes_{name}")
            z_scales = held([P, sum(widths)], U8, f"z_scales_{name}")
            c0 = 0
            for width in widths:
                nc.vector.quantize_mx(
                    out=z_codes[:, c0 : c0 + width].bitcast(FP8X4),
                    scales=z_scales[:, c0 : c0 + width],
                    in_=woven[:, PACK * c0 : PACK * (c0 + width)],
                )
                c0 = c0 + width
            return z_codes, z_scales

        z_low = held([P, PACK, NCMP], BF16, "z_low")

        def finish_low_tile(g, u, on=None, skip=0):
            z = held([P, NCMP], BF16, f"z{g}_{u}", on=on, skip=skip)
            hold_above_margin(g, u, 0, NCMP, z[:])
            for e in range(2):
                nc.sync.dma_start(out=z_low[64 * g : 64 * g + 64, 2 * e + u, :], in_=z[e:P:2, :])

        gather_words(0, 0, 2)
        load_w(0, 1, on="tab0")
        load_w(0, 2, on="tab0", skip=4 * KB)
        gather_words(1, 0, 2)
        tab.append(held([P, T], U16, "tab2", on="later_words", skip=1 * KB))
        load_tab(2)
        planes[0] = held([P, S], U8, "plane0", on="later_words")
        nc.vector.tensor_copy(out=planes[0][:], in_=tab_sc[:].indirect(offs_t[:]))
        for a in range(1, PASSES):
            nc.sync.dma_start(
                out=planes[a][0:MOVED_ROWS, :].bitcast(I32),
                in_=planes[0][4 * a : 4 * a + MOVED_ROWS, :].bitcast(I32),
            )
        load_w(1, 0, on="scale_rows")
        cast_w(0, 0, room=8 * KB)
        quantize_w(0, 0, scales_on="tab_sc", scales_skip=1536)
        load_w(1, 1, on="wb0_0_0")
        cast_w(0, 1)
        quantize_w(0, 1, scales_on="tab_sc", scales_skip=1536 + 256)
        cast_w(0, 2)
        region("last_codes", 2 * KB + 8 * KB)
        quantize_w(0, 2, scales_on="tab_sc", scales_skip=1536 + 512, codes_on="last_codes", codes_skip=1536)
        load_margin(0, on="wb0_2_0")
        gather_words(2, 0, 1, on="wb0_1_0")
        gather_words(2, 1, 2, on="wb0_1_0", skip=1 * KB)
        load_w(1, 2, on="tab2", skip=3840)
        load_w(2, 0, on="tab2", skip=3840 + 4 * KB)
        read_tile(0, 0)
        read_tile(0, 1)
        load_w(2, 1, on="last_codes", skip=2 * KB)

        cast_w(1, 0)
        cast_w(1, 1, on="tab2", skip=256 + 1536, copy=nc.vector.tensor_copy)
        quantize_w(1, 0, scales_on="tab2")
        quantize_w(1, 1)
        w4_sc = held([P, 2, N], U8, "w4_sc", on="tab2", skip=256)
        nc.vector.memset(w4_sc[:].rearrange("p b n -> p (b n)").bitcast(I32), 0)
        for q in range(4):
            nc.sync.dma_start(
                out=w4_sc[32 * q : 32 * q + 4].bitcast(I32),
                in_=w4_scales[:, 4 * q : 4 * q + 4, :].bitcast(I32).rearrange("b r c -> r b c"),
            )

        cast_w(1, 2, on="last_codes")
        cast_w(2, 0, on="w_raw1_2")

        pick_neighbour(0, 0, on="w_raw1_1")
        subtract(0, 0, room=8 * KB)
        load_w(2, 2, on="neighbour0_0_0")
        finish_low_tile(0, 0)
        load_margin(1, on="diff0_0_0")
        quantize_w(1, 2)
        read_tile(1, 0, on="w_raw2_0")
        cast_w(2, 1, u0=0, count=2, on="w_raw2_0", skip=4 * KB)
        read_tile(1, 1)
        cast_w(2, 2, u0=0, count=2, on="codes1_2_0")
        cast_w(2, 1, u0=2, count=2, on="codes1_1_0")

        pick_neighbour(0, 1, on="wb1_2_0")
        subtract(0, 1, room=8 * KB)
        quantize_w(2, 0)
        pick_neighbour(1, 0, on="w_raw2_0", skip=6 * KB)
        finish_low_tile(0, 1)
        load_margin(2, on="diff0_1_0")
        subtract(1, 0, room=3 * KB)
        gain_high = held([P, PACK], F32, "gain_high", on="neighbour1_0_0")
        nc.sync.dma_start(out=gain_high[:], in_=gain[K_PASS:H].rearrange("(p u) -> p u", u=PACK))
        gains.append(gain_high[:])
        quantize_w(2, 1)
        pick_neighbour(1, 1, on="wb2_1_0")
        quantize_w(2, 2)
        finish_low_tile(1, 0, on="wb2_2_0")
        w4 = held([P, 2, 2 * N], U8, "w4", on="diff1_0_0")
        nc.sync.dma_start(out=w4[:].bitcast(I32), in_=w4_words.bitcast(I32).rearrange("b p c -> p b c"))
        subtract(1, 1, on="wb2_2_0", skip=1 * KB)
        quantize_w(2, 1, u0=2)
        finish_low_tile(1, 1, on="w_raw2_1", skip=2 * KB)
        read_tile(2, 0)
        read_tile(2, 1)
        cast_w(2, 2, u0=2, count=2, on="w_raw2_1")
        pick_neighbour(2, 0, 0, HEAD_COLS)
        region("last_codes_high", 4 * KB)
        quantize_w(2, 2, u0=2, codes_on="last_codes_high")
        read_tile(2, 2)
        read_tile(2, 3)
        woven_low = weave(z_low[:], NCMP, nc.scalar.copy, "woven_low", on="last_codes_high")

        out_rows = out.rearrange("(i p) j -> p i j", p=P)
        out_tiles = N // P
        per_store = out_tiles // 2

        def second_product(j0, j1, low, high, stores):
            width = j1 - j0
            accs = [psum.tile([P, width], F32, name="acc2", tag=f"bank{i}") for i in range(out_tiles)]
            for b, (z_codes, z_scales), base in ((0, low, j0), (1, high, 0)):
                for i in range(out_tiles):
                    for c in range(0, width, P):
                        nc.tensor.matmul_mx(
                            out=accs[i][:, c : c + P],
                            lhsT=w4[:, b, 2 * P * i : 2 * P * (i + 1)].bitcast(FP4X4),
                            lhsT_scale=w4_sc[:, b, P * i : P * (i + 1)],
                            rhs=z_codes[:, base + c : base + c + P].bitcast(FP8X4),
                            rhs_scale=z_scales[:, base + c : base + c + P],
                            start=(b == 0 and c == 0),
                            stop=(b == 1 and c == width - P),
                        )
            for half, (copy, queue) in enumerate(stores):
                res = held([P, per_store, width], F32, f"res{j0}_{half}")
                for k in range(per_store):
                    copy(out=res[:, k, :], in_=accs[per_store * half + k][:])
                queue.dma_start(out=out_rows[:, per_store * half : per_store * (half + 1), j0:j1], in_=res[:])

        z_head = held([P, PACK, HEAD_COLS], BF16, "z_head")
        z_tail = held([P, PACK, NCMP - HEAD_COLS], BF16, "z_tail")

        for u in range(PACK):
            subtract(2, u, 0, HEAD_COLS)
            if u == PACK - 2:
                low = quantize_z(woven_low, (NCMP,), "low")
            if u < PACK - 1:
                pick_neighbour(2, u + 1, 0, HEAD_COLS, on={0: "w_raw2_2", PACK - 2: "z_low"}.get(u))
            else:
                pick_neighbour(2, 0, HEAD_COLS, NCMP)
            hold_above_margin(2, u, 0, HEAD_COLS, z_head[:, u, :])
        woven_head = weave(z_head[:], HEAD_COLS, nc.scalar.copy, "woven_head")

        for u in range(PACK - 2):
            subtract(2, u, HEAD_COLS, NCMP)
            pick_neighbour(2, u + 1, HEAD_COLS, NCMP)
            hold_above_margin(2, u, HEAD_COLS, NCMP, z_tail[:, u, :])
        subtract(2, PACK - 2, HEAD_COLS, NCMP)
        head = quantize_z(woven_head, (256, 128), "head")
        pick_neighbour(2, PACK - 1, HEAD_COLS, NCMP, on="z_head")
        hold_above_margin(2, PACK - 2, HEAD_COLS, NCMP, z_tail[:, PACK - 2, :])
        second_product(0, HEAD_COLS, low, head, ((nc.scalar.copy, nc.sync), (nc.scalar.copy, nc.sync)))
        subtract(2, PACK - 1, HEAD_COLS, NCMP)
        hold_above_margin(2, PACK - 1, HEAD_COLS, NCMP, z_tail[:, PACK - 1, :])

        woven_tail = weave(z_tail[:], NCMP - HEAD_COLS, nc.vector.tensor_copy, "woven_tail")
        tail = quantize_z(woven_tail, (NCMP - HEAD_COLS,), "tail")
        second_product(HEAD_COLS, NCMP, low, tail, ((nc.scalar.copy, nc.scalar), (nc.vector.tensor_copy, nc.sync)))
